import numpy as np, ml_dtypes
CORES = [6,15,38,47]
N = 4
BF = ml_dtypes.bfloat16
def gentries(a):
    return np.ascontiguousarray(a.reshape(8, 16, -1).transpose(0, 2, 1)).reshape(8, -1)
def gtable(e):
    e = np.asarray(e); return np.ascontiguousarray(e.reshape(8, -1, 16).transpose(0, 2, 1)).reshape(128, -1).astype(np.int32)
C, L, M, P, CAP, S, Q, RING = 64, 4096, 32, 512, 64, 2, 2, False
Z = 63 * S
def media(rng):
    return rng.integers(0, M, (N, 8, L)), rng.integers(-63, 64, (N, 8, 128 * M))
def zones(rng):
    t = rng.integers(CAP // 2, CAP + 1, (N, 8)); zr = rng.integers(0, t + 1)
    return np.roll(t - zr, 1, axis=0), zr, P - t - np.roll(t, 1, axis=0)
def crowd(rng, zl, zr, ni, near):
    n = zl + zr + ni; x = rng.integers(0, L, (N, 8, P))
    for r in range(N):
        for g in range(8):
            a = (near * rng.random(zl[r, g]) ** 2).astype(np.int64); b = L - 1 - (near * rng.random(zr[r, g]) ** 2).astype(np.int64)
            x[r, g, :n[r, g]] = rng.permutation(np.concatenate([a, b, rng.integers(Z, L - Z, ni[r, g])]))
    return x, n
def names(rng):
    return rng.integers(1, 2 ** 20, (N, 8, P)) * rng.choice(np.array([-1, 1]), (N, 8, P))
def pack(x, v, w, n, med, kick):
    d = {"x": np.stack([gtable(a) for a in x]), "v": np.stack([gtable(a) for a in v]), "w": np.stack([gtable(a) for a in w])}
    d["live"] = np.repeat(n, 16, axis=1)[:, :, None].astype(np.int32); d["med"] = med.astype(np.int32); d["kick"] = kick.astype(np.int32); return d
def plain(rng):
    zl, zr, room = zones(rng); x, n = crowd(rng, zl, zr, rng.integers(room // 3, room + 1), Z)
    return x, rng.integers(-63, 64, (N, 8, P)), names(rng), n
def setup_inputs(rng):
    return pack(*plain(rng), *media(rng))
def setup_inputs_full(rng):
    s = rng.permutation(np.array([1, 1, 1, 1, -1, -1, -1, -1])); right = np.where(s > 0, CAP, 0); left = CAP - right
    zr = np.tile(right, (N, 1)); zl = np.tile(left, (N, 1))
    if not RING:
        zr[N - 1] = 0; zl[0] = 0
    ni = P - zl - zr
    if not RING:
        ni[N - 1] -= right; ni[0] -= left
    x, n = crowd(rng, zl, zr, ni, 63); med, kick = media(rng); b = 63 * (S + 1)
    med[:, :, :b] = M - 1; med[:, :, L - b:] = M - 1
    for g in range(8):
        kick[:, g, 128 * (M - 1):] = 63 * s[g]
    return pack(x, rng.integers(-63, 64, (N, 8, P)), names(rng), n, med, kick)
def setup_inputs_both(rng):
    zl = np.full((N, 8), CAP); zr = np.full((N, 8), CAP)
    if not RING:
        zl[0] = 0; zr[N - 1] = 0
    x, n = crowd(rng, zl, zr, P - zl - zr, 63); med, kick = media(rng); b = 63 * (S + 1); e = 128 * (M - 1)
    med[:, :, :b] = M - 1; med[:, :, L - b:] = M - 1; kick[:, :, e:e + 64] = -63; kick[:, :, e + 64:] = 63
    side = np.where(x < 63, -1, np.where(x >= L - 63, 1, 0)); v = np.where(side == 0, rng.integers(-63, 64, x.shape), 63 * side); w = np.abs(names(rng))
    for r in range(N):
        for g in range(8):
            for s in (-1, 0, 1):
                k = np.flatnonzero(side[r, g] == s); w[r, g, k] = w[r, g, k] * rng.permutation(1 - 2 * (np.arange(k.size) & 1))
    return pack(x, v, w, n, med, kick)
def setup_inputs_empty(rng):
    x, v, w, n = plain(rng); o = rng.permutation(8); keep = rng.random((N, 8)) > 0.4; keep[:, o[2]] = True; n = np.where(keep, n, 0)
    n[:, o[:2]] = 0; n[rng.integers(0, N), o[0]] = 1
    return pack(x, v, w, n, *media(rng))
def setup_inputs_edges(rng):
    x, v, w, n = plain(rng); med, kick = media(rng); far = (x >= Z) & (x < L - Z)
    y = (x & -64) + 63 * rng.integers(0, 2, x.shape); x = np.where(far & (y >= Z) & (y < L - Z), y, x)
    x = np.where(far, x, np.where(x < Z, rng.choice(np.array([0, 0, 1, 62, 63, 64]), x.shape), L - 1 - rng.choice(np.array([0, 0, 1, 62, 63, 64]), x.shape)))
    v = rng.choice(np.array([-63, -1, 0, 1, 63]), v.shape); kick = np.where(rng.random(kick.shape) < 0.75, rng.choice(np.array([-63, -62, -1, 0, 1, 62, 63]), kick.shape), kick)
    s = rng.permutation(np.array([1, 1, 1, -1, -1, -1, 0, 0]))[None, :, None]; w = np.where(s == 0, w, np.abs(w) * s)
    return pack(x, v, w, n, med, kick)
def setup_inputs_spread(rng):
    zl, zr, room = zones(rng); x, n = crowd(rng, zl, zr, np.maximum(1, (room * rng.random((N, 8)) ** 4).astype(np.int64)), Z)
    w = np.minimum(np.exp2(20 * rng.random((N, 8, P))).astype(np.int64), 2 ** 20 - 1) * rng.choice(np.array([-1, 1]), (N, 8, P))
    v = np.rint(63 * (2 * rng.random((N, 8, P)) - 1) ** 5).astype(np.int64)
    med = np.repeat((M * rng.random((N, 8, L // 16)) ** 3).astype(np.int64), 16, axis=2); kick = np.rint(63 * (2 * rng.random((N, 8, 128 * M)) - 1) ** 3).astype(np.int64)
    return pack(x, v, w, n, med, kick)
def run(x, v, w, n, med, kick):
    worst, most = 0, int(n.max()); ri, gi = np.arange(N)[:, None, None], np.arange(8)[None, :, None]; sh = np.array([[L], [0], [0]])
    for s in range(S):
        on = np.arange(P) < n[:, :, None]; c = x >> 6
        ch = np.zeros((N, 8, C), np.int64); np.add.at(ch, (ri, gi, c), np.where(on, np.sign(w), 0))
        E = np.add.accumulate(ch.transpose(1, 0, 2).reshape(8, N * C), axis=1).reshape(8, N, C).transpose(1, 0, 2)
        u = np.clip(v + np.take_along_axis(E, c, axis=2), -63, 63)
        for i in range(Q):
            m = np.take_along_axis(med, (x + u) & (L - 1), axis=2); u = np.take_along_axis(kick, 128 * m + 64 + u, axis=2)
        x = x + u; v = u
        if not RING:
            k = x[0] < 0; x[0] = np.where(k, -1 - x[0], x[0]); v[0] = np.where(k, -v[0], v[0])
            k = x[N - 1] >= L; x[N - 1] = np.where(k, 2 * L - 1 - x[N - 1], x[N - 1]); v[N - 1] = np.where(k, -v[N - 1], v[N - 1])
        lf, rt = on & (x < 0), on & (x >= L); st = on & ~lf & ~rt
        worst = max(worst, int(np.sum(lf, axis=2).max()), int(np.sum(rt, axis=2).max()))
        t = np.stack([x, v, w]); new = np.zeros((3, N, 8, P), np.int64); cnt = np.zeros((N, 8), np.int64)
        for r in range(N):
            a, b = (r + N - 1) % N, (r + 1) % N
            for g in range(8):
                e = np.concatenate([t[:, r, g][:, st[r, g]], t[:, a, g][:, rt[a, g]] - sh, t[:, b, g][:, lf[b, g]] + sh], axis=1)
                most = max(most, e.shape[1]); cnt[r, g] = min(e.shape[1], P); new[:, r, g, :cnt[r, g]] = e[:, :P]
        x, v, w = new; n = cnt
    return x, v, w, worst, most
def state(x, v, w, live, med, kick):
    h = [np.stack([gentries(a) for a in z]).astype(np.int64) for z in (x, v, w)]
    return h + [live[:, ::16, 0].astype(np.int64), med.astype(np.int64), kick.astype(np.int64)]
def check_inputs(d):
    big = 2 ** 20 - 1
    bad = [k for k, lo, hi in (("x", 0, L - 1), ("v", -63, 63), ("w", -big, big), ("live", 0, P), ("med", 0, M - 1), ("kick", -63, 63)) if d[k].min() < lo or d[k].max() > hi]
    if (d["w"] == 0).any():
        bad.append("w")
    if (d["live"].reshape(N, 8, 16) != d["live"].reshape(N, 8, 16)[:, :, :1]).any():
        bad.append("live")
    if bad:
        return bad
    worst, most = run(*state(d["x"], d["v"], d["w"], d["live"], d["med"], d["kick"]))[3:]
    return (["leavers"] if worst > CAP else []) + (["places"] if most > P else [])
def reference(x, v, w, live, med, kick):
    xe, ve, we, worst, most = run(*state(x, v, w, live, med, kick))
    return {"yx": np.stack([gtable(a) for a in xe]).astype(np.float32), "yv": np.stack([gtable(a) for a in ve]).astype(np.float32), "yw": np.stack([gtable(a) for a in we]).astype(np.float32)}

from concourse.bass import DstId, RemoteDMATransfer
from concourse.mybir import AluOpType as Op, AxisListType, ActivationFunctionType as Fn

WIN = 4224
HW = 66
DJ, LJ = 768, 1408
NV1, NV2 = 12, 10
TURN = (False, False)
BF, F32, I32, U16 = "bfloat16", "float32", "int32", "uint16"

SCRATCH = {}
for _n, _w, _d in (
        ("xi", 32, I32), ("vi", 32, I32), ("wi", 32, I32), ("lvi", 4, I32), ("tabi", 512, I32), ("tabb", 512, BF),
        ("win", WIN, BF), ("ones", 128, BF), ("zs", 864, BF), ("pi", 16, I32), ("cols", 24, F32),
        ("k16", 40, F32), ("jw", 40, F32), ("thr", 72, F32), ("hq", 128, BF), ("hqh", 128, BF), ("dd", 160, BF),
        ("idb", 128, BF), ("idf", 128, F32), ("blk", 128, BF), ("nblk", 128, BF), ("upp", 128, BF), ("nupp", 128, BF),
        ("keep", 128, BF), ("ge", 128, BF), ("p14", 128, BF), ("ya", 160, BF), ("yb", 160, BF),
        ("rst", 80, BF), ("on", 32, F32), ("sg", 32, F32), ("s", 32, F32),
        ("ns", 32, F32), ("msg0", 48, BF), ("land0", 144, BF), ("xs0", 32, F32), ("xneg", 32, F32), ("nsx", 64, F32),
        ("xs", 80, F32), ("vb", 64, BF), ("hb", 32 * HW, BF), ("hs", 160, BF), ("ew", 160, BF), ("offs", 512, U16),
        ("ga", 640, BF), ("gk", 1296, BF), ("ub", 160, BF), ("pci", 96, I32), ("pc", 512, BF), ("st1", 528, BF),
        ("st2", 640, BF), ("st2f", 656, BF), ("fl", 240, BF), ("sc", 160, BF), ("mm", 80, F32), ("tmp", 320, F32),
        ("sl", 32, BF), ("sj", 192, F32), ("xraw", 32, F32), ("w2", 2048, BF), ("ms", 512, BF), ("ex", 48, BF),
        ("land1", 288, BF), ("land2", 288, BF), ("m63", 40, BF), ("m63q", 40, BF), ("dfix", 16, BF), ("al2", 48, BF),
        ("sa", 48, BF), ("b0", 40, F32), ("cj", 80, F32), ("dx", 32, BF), ("dv", 32, BF), ("dr", 8, F32),
        ("tq", 288, BF), ("rq", 288, BF), ("trow", 128, BF), ("key", 192, BF), ("le", 160, BF), ("lc", 160, BF),
        ("oh", 128, BF), ("kk", 16, BF), ("tr2", 256, BF), ("trl", 640, BF), ("jh", 8, F32),
        ("ox", 32, F32), ("ov", 32, F32), ("ow", 32, F32)):
    SCRATCH[_n] = ("sbuf", [128, _w], _d)
SCRATCH["tr"] = ("sbuf", [128, 16, 32], BF)
BANKS = ("pU", "pA", "pB", "pH", "pR", "pQ", "pC", "pM")
for _n in BANKS:
    SCRATCH[_n] = ("psum", [128, 16, 32] if _n == "pR" else [128, 512], F32)

SEMAPHORES = ["cV", "cS", "cP", "cG", "ls", "ar0", "ar1", "ar1x", "ar2l", "ar2r", "ar2x"] + ["d%d" % _i for _i in range(16)]


def emit(g, T, ops):
    eng = {"V": g.vector, "S": g.scalar, "P": g.tensor, "G": g, "Y": g.sync}

    def hit(a, b):
        if len(a) == 4 == len(b) and a[3] == b[3] and (a[1] - b[1]) % a[3]:
            return False
        return a[0] == b[0] and a[1] < b[2] and b[1] < a[2]

    seq = {}
    for o in ops:
        seq[o["q"]] = seq.get(o["q"], 0) + 1
        o["seq"] = seq[o["q"]]
        o["banks"] = set(r[0] for r in o["r"] + o["w"] if r[0] in BANKS)
        o["names"] = set(r[0] for r in o["r"] + o["w"])
    known = {q: {} for q in eng}
    for n, o in enumerate(ops):
        if o["k"] == "x":
            o["clock"] = {("t", n): 1}
            continue
        kn = known[o["q"]]
        o["waits"] = []
        for m in range(n - 1, -1, -1):
            e = ops[m]
            if e["k"] == "r" or not (o["names"] & e["names"]):
                continue
            key, val = (e["q"], e["seq"]) if e["k"] == "c" else (("t", m), 1)
            if kn.get(key, 0) >= val:
                continue
            if e["q"] == "P" and o["q"] == "P":
                continue
            dep = e["q"] != o["q"] and bool(o["banks"] & e["banks"])
            dep = dep or any(hit(a, b) for a in o["r"] + o["w"] for b in e["w"])
            dep = dep or any(hit(a, b) for a in o["w"] for b in e["r"])
            if dep:
                o["waits"].append(m)
                e["inc"] = True
                for kk, vv in e["clock"].items():
                    if kn.get(kk, 0) < vv:
                        kn[kk] = vv
        o["clock"] = dict(kn)
        if o["k"] == "c":
            o["clock"][o["q"]] = o["seq"]
        else:
            o["clock"][("t", n)] = 1
    cnt = {}
    ndma = 0
    tail = []
    for o in ops:
        if o["k"] == "c" and o.get("inc"):
            cnt[o["q"]] = cnt.get(o["q"], 0) + 1
            o["tok"] = ("c" + o["q"], cnt[o["q"]])
        elif o["k"] == "d":
            o["tok"] = ("d%d" % ndma, 16)
            ndma += 1
        if o["k"] in "dx" and not o.get("inc"):
            tail.append(o)
    sent = 0
    for o in ops:
        if o["k"] == "x":
            continue
        for m in o["waits"]:
            eng[o["q"]].wait_ge(T.sem[ops[m]["tok"][0]], ops[m]["tok"][1])
        ins = o["f"]()
        if o["k"] == "d":
            ins.then_inc(T.sem[o["tok"][0]], 16)
        elif o["k"] == "r":
            sent += o["n"]
        elif o.get("inc"):
            ins.then_inc(T.sem[o["tok"][0]], 1)
    if sent:
        g.wait_ge(T.sem.ls, sent)
    for o in tail:
        g.wait_ge(T.sem[o["tok"][0]], o["tok"][1])


def rank_program(g, core, T, topo):
    rank = T.rank_of(core)
    if rank is None:
        return
    N = len(T.cores)
    hasL, hasR = rank > 0, rank < N - 1
    nd = int(hasL) + int(hasR)
    dirs = ([-1] if hasL else []) + ([1] if hasR else [])
    ops = []
    V, S, P = g.vector, g.scalar, g.tensor

    def A(name, lo=0, hi=None, step=1):
        t = T[name]
        hi = t.shape[1] if hi is None else hi
        return (t[:, lo:hi] if step == 1 else t[:, lo:hi:step], (name, lo, hi, step))

    def rec(q, f, r, w, k="c", **kw):
        o = {"q": q, "f": f, "r": [a[1] for a in r if isinstance(a, tuple)], "w": [a[1] for a in w], "k": k}
        o.update(kw)
        ops.append(o)

    def ap(a):
        return a[0] if isinstance(a, tuple) else a

    def memset(o, c):
        rec("V", lambda: V.memset(o[0], c), [], [o])

    def copy(o, i):
        rec("V", lambda: V.tensor_copy(o[0], i[0]), [i], [o])

    def ts(o, i, a, op0, b=None, op1=None):
        if op1 is None:
            rec("V", lambda: V.tensor_scalar(o[0], i[0], ap(a), None, op0), [i, a], [o])
        else:
            rec("V", lambda: V.tensor_scalar(o[0], i[0], ap(a), ap(b), op0, op1), [i, a, b], [o])

    def tt(o, a, b, op):
        rec("V", lambda: V.tensor_tensor(o[0], a[0], b[0], op), [a, b], [o])

    def red(o, i):
        rec("V", lambda: V.tensor_reduce(o[0], i[0], AxisListType.X, Op.add), [i], [o])

    def scan(o, d0, d1, init):
        rec("V", lambda: V.tensor_tensor_scan(o[0], d0[0], d1[0], init, Op.mult, Op.add), [d0, d1], [o])

    def turn(o, i):
        rec("V", lambda: V.transpose(o[0], i[0]), [i], [o])

    def act(o, i, fn=Fn.Copy, bias=None, scale=None, acc=None):
        kw = {}
        if bias is not None:
            kw["bias"] = ap(bias)
        if scale is not None:
            kw["scale"] = ap(scale)
        if acc is not None:
            kw["accum_out"] = acc[0]
        rec("S", lambda: S.activation(o[0], i[0], fn, **kw), [i, bias, scale], [o] + ([acc] if acc else []))

    def zero(name, lo, hi):
        act(A(name, lo, hi), A("tabb", 0, hi - lo), scale=0.0)

    def mm(o, l, r, start, stop):
        rec("P", lambda: P.matmul(o[0], l[0], r[0], start, stop), [l, r], [o])

    def dma(q, o, i):
        e = g.sync if q == "Y" else g.scalar
        rec(q, lambda: e.dma_start(ap(o), ap(i)), [i], [o] if isinstance(o, tuple) else [], k="d")

    def iota(o, pat, base, cm, flt=True):
        if flt:
            rec("G", lambda: g.iota(o[0], pat, base, cm, allow_small_or_imprecise_dtypes=True), [], [o])
        else:
            rec("G", lambda: g.iota(o[0], pat, base, cm), [], [o])

    def sel(o, i, pat, cmp, fill, base, cm):
        rec("G", lambda: g.affine_select(o[0], i[0], pat, cmp, fill, base, cm), [i], [o])

    def send(items, per):
        trs = []
        for n, (dst, src, land, sem) in enumerate(items):
            dc = T.cores[dst]
            es = topo.engines(core, dc)[n * per:(n + 1) * per]
            rid, pid = topo.addr(dc)[:2]
            trs.append(RemoteDMATransfer(dst_ids=[DstId(rid=rid, pnc=pid)], dma_engine_mask=sum(1 << e for e in es),
                                         remote_sem=T.sem[sem], src=src[0], dst=land[0]))
        rec("G", lambda: g.remote_dma_fused(trs, local_sem=T.sem.ls), [it[1] for it in items], [], k="r",
            n=per * len(items))

    def arrive(land, sem, n):
        rec("G", None, [], land, k="x", tok=(sem, n))

    ZE, ZMED, ZKICK, ZXV, ZW, ZI = range(6)

    def conv(bank, lo, hi, z, src, base, start, stop):
        n = hi - lo
        for i in range(16):
            mm(A(bank, lo, hi), A("zs", z * 144 + 15 - i, z * 144 + 143 - i), A(src, base + i, base + 16 * n, 16),
               start and i == 0, stop and i == 15)

    def half(kk, h):
        lo = 16 + 16 * (kk - h)
        return A("yb" if kk else "ya", lo, lo + 128)

    def convt(bank, lo, hi, c, src, base, start, stop):
        for kk in range(2):
            for h in range(2):
                mm(A(bank, lo + kk, hi, 2), half(kk, h), A(src, base + 16 * h + c, base + 16 * (hi - lo), 32),
                   start and kk + h == 0, stop and kk + h == 2)

    PR, TR = (T.pR[:], ("pR", 0, 512)), (T.tr[:], ("tr", 0, 512))

    def rows(stop):
        for kk in range(2):
            for h in range(2):
                mm((T.pR[:, :, 16 * kk:16 * kk + 16], PR[1]), half(kk, h), (T.tr[:, :, 16 * h:16 * h + 16], TR[1]),
                   kk + h == 0, stop and kk + h == 2)

    def pickv(o, win, f):
        rec("V", lambda: V.tensor_copy(o[0], win[0].indirect(f[0])), [win, f], [o])

    def picks(o, win, f):
        rec("S", lambda: S.activation(o[0], win[0].indirect(f[0]), Fn.Copy), [win, f], [o])

    def gather(win, off, W, out, ob):
        h = W // 2
        pickv(A(out, ob, ob + 16 * h), win, A("offs", off, off + h))
        picks(A(out, ob + 16 * h, ob + 16 * W), win, A("offs", off + h, off + W))

    def scatter(win, off, a, b, op):
        rec("V", lambda: V.tensor_tensor(win[0].indirect(off[0]), a[0], b[0], op), [off, a, b], [win])

    def zv(s, n=143):
        return A("zs", s * 144 + 15, s * 144 + n, 16)

    def col(n):
        return A("cols", n, n + 1)

    def pc(c):
        return A("pc", c, 512, 16)

    def run(fs):
        for f in fs:
            f()

    thr = A("thr", 0, HW)

    def hist(xb, nb, nv):
        hv = [lambda k=k: ts(A("hb", k * HW, (k + 1) * HW), thr, A(xb, k, k + 1), Op.is_ge, A("s", k, k + 1), Op.mult)
              for k in range(nv)]
        hs = [lambda k=k: act(A("hb", k * HW, (k + 1) * HW), thr, Fn.Sign, bias=A("nsx", nb + k, nb + k + 1),
                              scale=A("s", k, k + 1)) for k in range(nv, 32)]
        return hv, hs

    def hist_sum(nv, hsb):
        lead = 32 - 2 * nv
        order = list(range(nv, nv + lead))
        for k in range(nv):
            order += [nv + lead + k, k]
        for n, k in enumerate(order):
            mm(A("pH", 0, HW), A("hq" if k < nv else "hqh"), A("hb", k * HW, (k + 1) * HW), n == 0, n == 31)
            if n == lead - 1:
                mm(A("pH", 0, HW), A("hqh"), A("hs", hsb, hsb + HW), False, False)

    dma("Y", A("wi"), T.w[:])
    dma("S", A("lvi", 0, 1), T.live[:])
    dma("Y", A("xi"), T.x[:])
    dma("S", A("tabi", 256, 512), T.kick[:])
    dma("Y", A("tabi", 0, 256), T.med[:])
    dma("S", A("vi"), T.v[:])
    memset(A("win", 0, 704), 0.0)
    memset(A("ones"), 1.0)
    act(A("win", 704, 1408), A("win", 0, 704))
    act(A("win", 1408, 2112), A("win", 0, 704))
    act(A("win", 2112, 2464), A("win", 0, 352))
    act(A("zs", 144, 848), A("win", 0, 704))
    memset(A("win", 2464, WIN), 0.0)
    iota(A("pi", 0, 1), [[0, 1]], 0, 1, False)
    iota(A("k16"), [[16, 40]], 0, 0)
    iota(thr, [[64, HW]], 63 - 2048, 0)
    iota(A("dd"), [[-1, 160]], 16, 1)
    sel(A("hq"), A("ones"), [[-16, 8], [-4, 16]], Op.is_ge, 0.0, 0, 1)
    sel(A("hq"), A("hq"), [[16, 8], [4, 16]], Op.is_ge, 0.0, 3, -1)
    ts(A("pi", 4, 5), A("pi", 0, 1), 15, Op.bitwise_and)
    memset(A("zs", 0, 144), 0.0)
    copy(col(0), A("pi", 4, 5))
    ts(thr, thr, 0.5, Op.add)
    ts(A("jw"), A("k16"), col(0), Op.add)
    if not hasR:
        memset(A("thr", 63, HW), 65536.0)
    ts(A("idb"), A("dd", 16, 144), 0.0, Op.is_equal)
    ts(A("pi", 8, 9), A("pi", 0, 1), 16, Op.bitwise_and)
    ts(A("ge"), A("dd", 16, 144), 0.0, Op.is_ge)
    ts(col(9), A("pi", 8, 9), 0.0, Op.is_equal)
    ts(col(10), A("pi", 8, 9), 0.0, Op.not_equal)
    memset(A("zs", 848, 864), 0.0)
    copy(col(1), A("lvi", 0, 1))
    ts(A("sg"), A("wi"), -1.0, Op.max, 1.0, Op.min)
    ts(A("on"), A("jw", 0, 32), col(1), Op.is_lt)
    ts(A("xneg"), A("xi"), -1.0, Op.mult, 2048.0, Op.add)
    tt(A("s"), A("sg"), A("on"), Op.mult)
    ts(A("hqh"), A("hq"), 0.5, Op.mult)
    per0 = [2, 4, 4]
    if hasR:
        red(col(2), A("s"))
    tt(A("nsx", 0, 32), A("xneg"), A("s"), Op.mult)
    if hasR:
        ts(A("msg0", 0, 40), A("k16"), 0.0, Op.mult, col(2), Op.add)
        send([(d, A("msg0", 0, 40), A("land0", 48 * rank, 48 * rank + 40), "ar0") for d in range(rank + 1, N)], per0[rank])
    if hasL:
        arrive([A("land0")], "ar0", sum(per0[:rank]))
    sel(A("blk"), A("ones"), [[-16, 8], [0, 16]], Op.is_ge, 0.0, 0, 1)
    sel(A("blk"), A("blk"), [[16, 8], [0, 16]], Op.is_ge, 0.0, 15, -1)
    iota(A("tq", 0, 128), [[16, 4], [0, 32]], 64, 0)
    iota(A("tq", 128, 288), [[16, 4], [0, 40]], 64, 0)
    iota(A("trow"), [[-64, 2], [1, 64]], 65, 0)
    sel(zv(ZXV), A("ones", 0, 8), [[-16, 8]], Op.is_ge, 0.0, -1, 1)
    sel(zv(ZXV), zv(ZXV), [[16, 8]], Op.is_ge, 0.0, 5, -1)
    sel(zv(ZW), A("ones", 0, 8), [[-16, 8]], Op.is_ge, 0.0, -7, 1)
    sel(zv(ZW), zv(ZW), [[16, 8]], Op.is_ge, 0.0, 9, -1)
    hv, hs = hist("xs0", 0, NV1)
    run(hs)
    red(col(3), A("s", NV1, 32))
    ts(A("tabb", 0, 256), A("tabi", 0, 256), 128.0, Op.mult)
    dma("Y", (T.win[0::16, 64:4160], ("win", 64, 4160)), A("tabb", 0, 256))
    dma("Y", (T.win[0::16, 0:64], ("win", 0, 64)), (T.tabb[15::16, 192:256], ("tabb", 192, 256)))
    dma("Y", (T.win[0::16, 4160:WIN], ("win", 4160, WIN)), (T.tabb[0::16, 0:64], ("tabb", 0, 64)))
    ts(A("hs", 0, HW), thr, 0.0, Op.mult, col(3), Op.add)
    ts(A("xs0"), A("xi"), 2048.0, Op.subtract)
    copy(A("tabb", 256, 512), A("tabi", 256, 512))
    dma("Y", (T.win[1::16, 0:4096], ("wink", 0, 4096)), A("tabb", 256, 512))
    run(hv)
    ts(A("offs", 0, 32), A("xi"), -31.5, Op.add, 1.0 / 64, Op.mult)
    copy(A("vb", 0, 32), A("vi"))
    copy(zv(ZE), A("hq", 0, 128, 16))
    act(A("idf"), A("idb"))
    hist_sum(NV1, 0)
    copy(A("ew", 0, HW), A("pH", 0, HW))
    gather(A("ew", 0, HW), 0, 32, "ga", 0)
    conv("pU", 0, 32, ZE, "ga", 0, True, False)
    mm(A("pU", 0, 32), A("idb"), A("vb", 0, 32), False, not hasL)
    zero("pc", 0, 512)
    act(pc(6), A("xs0"), Fn.Sign, bias=0.5)
    zero("key", 0, 192)
    zero("ex", 0, 48)
    tt(A("xs", 0, 32), A("xs0"), A("on"), Op.mult)
    copy(zv(ZMED), A("idb", 0, 128, 16))
    copy(zv(ZKICK), A("idb", 1, 128, 16))
    ts(A("pci", 0, 32), A("xi"), 2048.0, Op.add)
    ts(A("ya"), A("dd"), 0.0, Op.is_equal, col(9), Op.mult)
    ts(A("pci", 32, 64), A("pci", 0, 32), 4095, Op.bitwise_and)
    ts(A("yb"), A("dd"), 0.0, Op.is_equal, col(10), Op.mult)
    memset(A("rst"), 1.0)
    red(col(4), A("s", NV2, 32))
    memset(A("rq"), 1.0)
    mm(A("pA", 0, 32), A("idf"), A("xs", 0, 32), True, False)
    for r in range(rank):
        mm(A("pU", 0, 32), A("blk"), A("land0", 48 * r, 48 * r + 32), False, r == rank - 1)

    WT = (T.win[:, :], ("win", 0, WIN))

    def look(off, W, out, ob, fill, bank, c, start, stop, tn):
        gather(WT, off, W, out, ob)
        ops[-1]["r"].append(("wink", 0, 4096))
        ops[-2]["r"].append(("wink", 0, 4096))
        if tn:
            turn(A("trl", 0, 16 * W), A(out, ob, ob + 16 * W))
        run(fill)
        if tn:
            convt(bank, 0, W, c, "trl", 0, start, stop)
        else:
            conv(bank, 0, W, ZMED + c, out, ob, start, stop)

    def chain(W, xb, ob, ub, gb, pf, vf, tn):
        xs, u0, u1 = A("xs", xb, xb + W), A("ub", ub, ub + W), A("ub", ub + 40, ub + 40 + W)
        pa, pb = A("pA", 0, W), A("pB", 0, W)
        ts(A("offs", ob, ob + W), pa, 2112.0, Op.add)
        run(pf[0])
        look(ob, W, "ga", 0, vf[0], "pB", 0, True, False, tn)
        mm(pb, A("idb"), u0, False, True)
        ts(A("offs", ob + 40, ob + 40 + W), pb, 64.0, Op.add)
        mm(pa, A("idf"), xs, True, False)
        run(pf[1])
        look(ob + 40, W, "ga", 0, vf[1], "pA", 1, False, True, tn)
        ts(A("offs", ob + 80, ob + 80 + W), pa, 2112.0, Op.add)
        run(pf[2])
        look(ob + 80, W, "ga", 0, [lambda: tt(u1, pa, xs, Op.subtract)] + vf[2], "pB", 0, True, False, tn)
        mm(pb, A("idb"), u1, False, True)
        ts(A("offs", ob + 120, ob + 120 + W), pb, 64.0, Op.add)
        mm(pa, A("idf"), xs, True, False)
        run(pf[3])
        look(ob + 120, W, "gk", gb, vf[3], "pA", 1, False, True, tn)

    def pack(W, fb, sb, kb, tb, ob, gb, st, mb, f_scan, f_pe, f_cnt, f_conv):
        pa, n = A("pA", 0, W), nd * W
        fl, sc = A("fl", fb, fb + n), A("sc", sb, sb + n)
        for d, sd in enumerate(dirs):
            ts(A("fl", fb + d * W, fb + (d + 1) * W), pa, -2048.0 if sd < 0 else 2047.0, Op.is_lt if sd < 0 else Op.is_gt)
        mm(A("pM", 0, n), A("nupp"), fl, True, False)
        mm(A("pM", 0, n), A("idb"), fl, False, False)
        scan(sc, A("rst", 40 - W, 40 - W + n), fl, 4.0)
        run(f_scan)
        mm(A("pM", 0, n), A("blk"), sc, False, True)
        for q in range(4):
            mm(A("pQ", q * W, (q + 1) * W), A("blk"), A("sc", sb, sb + W), True, True)
        if nd == 2:
            mm(A("pC", 0, W), A("blk"), A("sc", sb + W, sb + n), True, True)
        mm(A("pC", 48, 49), A("blk"), A("sc", sb + W - 1, sb + W), True, True)
        run(f_pe)
        if nd == 2:
            for q in range(4):
                act(A("sj", 48 * q, 48 * q + W), A("pC", 0, W), Fn.Sign, bias=A("jh", q, q + 1), scale=-1.0, acc=col(16 + q))
        tt(A("key", kb, kb + n), A("pM", 0, n), fl, Op.mult)
        tt(A("le", 0, 4 * W), A("pQ", 0, 4 * W), A("tq", tb, tb + 4 * W), Op.is_le)
        scan(A("lc", 0, 4 * W), A("rq", tb, tb + 4 * W), A("le", 0, 4 * W), 0.0)
        k0 = A("lc", W - 1, 4 * W, W)
        copy(A("offs", ob, ob + 4), k0)
        if nd == 2:
            ts(A("offs", ob + 4, ob + 8), A("cols", 16, 20), 0.5, Op.mult, 1.5 * W, Op.add)
        run(f_cnt)
        kw, ko, oh, tw = A("key", kb, kb + n + 1), A("offs", ob, ob + 4 * nd), A("oh", 0, 64 * nd), A("trow", 0, 64 * nd)
        rec("V", lambda: V.tensor_tensor(oh[0], kw[0].indirect(ko[0]), tw[0], Op.is_equal), [kw, ko, tw], [oh])
        ts(A("kk", 0, 4), k0, 16.0, Op.mult)
        if nd == 2:
            ts(A("kk", 4, 8), A("cols", 16, 20), 8.0, Op.mult, 8.0 * W, Op.add)
        conv("pB", 0, 4 * nd, ZI, "oh", 0, True, False)
        mm(A("pB", 0, 4 * nd), A("idb"), A("kk", 0, 4 * nd), False, True)
        run(f_conv)
        so = A("offs", ob + 8, ob + 8 + 4 * nd)
        copy(so, A("pB", 0, 4 * nd))
        pickv(A("ms", mb, mb + 64 * nd), A(st, 0, 16 * W + 16), so)
        picks(A("ms", mb + 128, mb + 128 + 64 * nd), A("gk", gb, gb + 16 * W + 16), so)

    def migrate(mb, land, sems):
        items = []
        for d, sd in enumerate(dirs):
            lo = 16 if sd > 0 else 80
            for part in (0, 128):
                items.append((rank + sd, A("ms", mb + part + 64 * d, mb + part + 64 * d + 64),
                              A(land, lo + part, lo + part + 64), sems[sd > 0]))
        send(items, 4 // nd)

    def comes(src):
        return 8 if src in (0, N - 1) else 4

    def stays(W, fb):
        o = A("fl", fb + nd * W, fb + (nd + 1) * W)
        if nd == 2:
            tt(o, A("fl", fb, fb + W), A("fl", fb + W, fb + 2 * W), Op.is_equal)
        else:
            ts(o, A("fl", fb, fb + W), 0.0, Op.is_equal)

    ts(A("ub", 0, 32), A("pU", 0, 32), -63.0, Op.max, 63.0, Op.min)
    mm(A("pA", 0, 32), A("idb"), A("ub", 0, 32), False, True)
    vf = [[lambda: copy(pc(7), A("wi")), lambda: copy(pc(2), A("pci", 32, 64)),
           lambda: tt(A("tmp", 0, 32), A("wi"), pc(7), Op.subtract), lambda: tt(pc(3), A("pci", 32, 64), pc(2), Op.subtract),
           lambda: copy(pc(8), A("tmp", 0, 32)), lambda: ts(pc(10), A("pci", 32, 64), 2048.0, Op.subtract),
           lambda: tt(pc(9), A("tmp", 0, 32), pc(8), Op.subtract), lambda: memset(A("rst", 40, 41), 0.0),
           lambda: zero("w2", 0, 512)],
          [lambda: turn(TR, A("pc")), lambda: tt(A("upp"), A("ge"), A("blk"), Op.mult),
           lambda: memset(A("rq", 0, 128, 32), 0.0), lambda: memset(A("rq", 128, 288, 40), 0.0),
           lambda: act(A("ns"), A("s"), scale=-1.0), lambda: act(A("tq"), A("tq"), Fn.Identity, bias=col(0)),
           lambda: act(zv(ZI), A("blk", 0, 128, 16), scale=col(0)),
           lambda: act(A("jh", 0, 4), A("jw", 0, 4), Fn.Identity, bias=0.5)],
          [lambda: memset(A("offs", 232, 236), 0), lambda: memset(A("offs", 236, 240), 63),
           lambda: ts(col(6), col(0), 6.0, Op.is_equal, -2.0, Op.mult), lambda: memset(A("gk", 512, 528), 0.0),
           lambda: memset(A("st1", 512, 528), 0.0), lambda: ts(col(8), col(6), 1.0, Op.add),
           lambda: ts(col(7), col(0), 1.0, Op.is_equal),
           lambda: act(A("nupp"), A("upp"), scale=-1.0),
           lambda: act(A("hs", 80, 80 + HW), thr, Fn.Identity, bias=col(4), scale=0.0),
           lambda: act(A("nblk"), A("blk"), scale=-1.0), lambda: act(zv(ZXV), zv(ZXV), scale=128.0),
           lambda: sel(zv(ZXV), zv(ZXV), [[-16, 8]], Op.not_equal, 129.0, -1, 1),
           lambda: sel(zv(ZXV), zv(ZXV), [[-16, 8]], Op.not_equal, 2048.0 * 128, -6, 1)],
          [lambda: ts(A("p14"), A("dd", 13, 141), 0.0, Op.is_equal, col(7), Op.mult),
           lambda: memset(A("m63", 32, 36), 0.0), lambda: memset(A("m63", 36, 40), 1.0),
           lambda: ts(A("keep"), A("idb"), col(8), Op.mult), lambda: memset(A("gk", 1280, 1296), 0.0),
           lambda: memset(A("st2f", 640, 656), 0.0), lambda: act(A("st1", 0, 512), PR)]]
    chain(32, 0, 40, 0, 0, [[], [], [lambda: rows(True)], []], vf, TURN[0])
    hv, hs = hist("xraw", 32, NV2)
    nl1 = A("fl", nd * 32, nd * 32 + 32)

    def counts1():
        small = []
        for d, sd in enumerate(dirs):
            e = 0 if sd < 0 else 16
            if d == 0:
                act(A("ex", e, e + 1), A("pC", 48, 49), Fn.Identity, bias=-64.0)
            else:
                act(A("ex", e, e + 1), A("pC", 31, 32))
            small.append((rank + sd, A("ex", e, e + 8), A("land1", 272, 280) if sd < 0 else A("land1", 0, 8), "ar1x"))
        if hasL:
            act(A("sj", 0, 32), A("pB", 64, 96), acc=col(5))
            act(A("ex", 1, 2), col(5))
        send(small, 4)
        run(hs[:16])

    pack(32, 0, 0, 0, 0, 240, 0, "st1", 0,
         [lambda: act(A("xraw"), A("pA", 0, 32))] + ([lambda: tt(A("sl"), A("fl", 0, 32), A("s"), Op.mult)] if hasL else [])
         + [lambda: tt(A("nsx", 32, 64), A("xraw"), A("ns"), Op.mult)],
         [lambda: mm(A("pB", 64, 96), A("blk"), A("sl"), True, True)] if hasL else [],
         [counts1], hv[:6])
    migrate(0, "land1", ("ar1", "ar1"))
    run(hs[16:])
    run(hv[6:])
    ts(A("offs", 200, 232), A("xraw"), 2048.0 - 31.5, Op.add, 1.0 / 64, Op.mult)
    v2, x2 = A("vb", 32, 64), A("xs", 40, 72)
    hist_sum(NV2, 80)
    if nd == 2:
        mm(PR, A("idb"), A("st1", 0, 512), True, False)
        mm(PR, A("p14"), A("gk", 0, 512), False, True)
    stays(32, 0)
    tt(v2 if nd == 2 else A("tmp", 96, 128), A("xraw"), A("xs", 0, 32), Op.subtract)
    copy(A("ew", 80, 80 + HW), A("pH", 0, HW))
    gather(A("ew", 80, 80 + HW), 200, 40, "ga", 0)
    conv("pU", 0, 40, ZE, "ga", 0, True, False)
    tt(A("al2", 0, 32), A("on"), nl1, Op.mult)
    if hasR:
        ts(A("m63", 0, 32), A("xraw"), 1984.0, Op.is_ge)
    if nd == 2:
        tt(x2, A("xraw"), A("al2", 0, 32), Op.mult)
    else:
        lim, cmp, c = (2047.0, Op.is_gt, 4095.0) if hasL else (-2048.0, Op.is_lt, -4097.0)
        ts(A("tmp", 128, 160), A("xraw"), -2.0, Op.mult, c, Op.add)
        ts(A("tmp", 160, 192), A("xraw"), lim, cmp)
        ts(A("tmp", 192, 224), A("xraw"), lim, cmp, -2.0, Op.mult)
        tt(A("dx"), A("tmp", 128, 160), A("tmp", 160, 192), Op.mult)
        tt(A("dv"), A("tmp", 96, 128), A("tmp", 192, 224), Op.mult)
        tt(A("tmp", 224, 256), A("xraw"), A("dx"), Op.add)
        tt(v2, A("tmp", 96, 128), A("dv"), Op.add)
        for lo, hi in (((80, 144), (208, 288)) if hasL else ((0, 80), (144, 208))):
            zero("land1", lo, hi)
        tt(x2, A("tmp", 224, 256), A("al2", 0, 32), Op.mult)
    arrive(([A("land1", 0, 8)] if hasL else []) + ([A("land1", 272, 280)] if hasR else []), "ar1x", 4 * nd)
    if hasR:
        ts(A("m63q"), A("m63"), A("land1", 273, 274), Op.mult)
    ts(A("dfix", 0, 4), A("jw", 0, 4), A("land1", 0, 1), Op.is_lt, -2048.0, Op.mult)
    ts(A("dfix", 4, 8), A("jw", 0, 4), A("land1", 272, 273), Op.is_lt, 2048.0, Op.mult)
    mm(A("pU", 0, 32), A("idb"), v2, False, False)
    for r in range(rank):
        mm(A("pU", 0, 40), A("blk"), A("land0", 48 * r, 48 * r + 40), False, False)
    if hasR:
        mm(A("pU", 0, 40), A("idb"), A("m63q"), False, False)
    mm(A("pA", 0, 32), A("idf"), x2, True, False)
    mm(A("pA", 32, 40), A("idb"), A("dfix", 0, 8), False, False)
    if nd == 2:
        act(A("st2", 0, 512), PR)
    zones = ([16] if hasL else []) + ([80] if hasR else [])
    arrive([A("land1", lo + part, lo + part + 64) for lo in zones for part in (0, 128)], "ar1",
           sum(comes(rank + sd) for sd in dirs))
    turn(A("tr2"), A("land1", 16, 272))
    convt("pU", 32, 40, 1, "tr2", 128, False, True)
    convt("pA", 32, 40, 1, "tr2", 128, False, False)
    convt("pA", 32, 40, 10, "tr2", 0, False, False)
    ts(A("ub", 80, 120), A("pU", 0, 40), -63.0, Op.max, 63.0, Op.min)
    mm(A("pA", 0, 40), A("idb"), A("ub", 80, 120), False, True)
    bb = nd * 40
    end = nd == 1
    pf = [[lambda: mm(A("pM", 0, 128), A("keep"), A("land1", 16, 144), True, False),
           lambda: mm(A("pM", 0, 128), A("p14"), A("land1", 144, 272), False, True)],
          [lambda: mm(A("pH", 0, 40), A("blk"), A("sa", 0, 40), True, False),
           lambda: mm(A("pH", 0, 40), A("nupp"), A("al2", 0, 40), False, True)],
          [lambda: rows(False), lambda: mm(PR, A("p14"), A("gk", 0, 512), False, True)] if end else [],
          [lambda: mm(A("pH", 0, 40), A("idf"), A("b0"), True, False)]]
    vf = [[lambda: tt(A("xs", 72, 80), A("pA", 32, 40), A("ub", 112, 120), Op.subtract),
           lambda: ts(A("al2", 32, 40), A("dfix", 0, 8), 0.0, Op.not_equal),
           lambda: scan(A("sa", 0, 40), A("ones", 0, 40), A("al2", 0, 40), 0.0),
           lambda: act(A("st2", 512, 640), A("pM", 0, 128)),
           lambda: act(A("cj", 0, 40), A("jw"), Fn.Identity, bias=-float(DJ), scale=-1.0),
           lambda: act(A("cj", 40, 80), A("jw"), Fn.Identity, bias=float(LJ)), lambda: zero("w2", 512, 640)]
          + ([lambda: copy(pc(5), A("dx"))] if end else []),
          [lambda: tt(A("tmp", 256, 296), A("pH", 0, 40), A("cj", 0, 40), Op.add)]
          + ([lambda: turn(TR, A("pc"))] if end else [lambda: act(A("st2f", 0, 512), A("st2", 0, 512), scale=col(8))]),
          [lambda: tt(A("mm", 0, 40), A("tmp", 256, 296), A("al2", 0, 40), Op.mult),
           lambda: ts(A("b0"), A("mm", 0, 40), float(DJ - LJ + 64), Op.add)]
          + ([lambda: act(A("st2", 0, 512), PR)] if end else [lambda: act(A("st2f", 512, 640), A("st2", 512, 640), scale=col(8))]),
          [lambda: act(A("st2f", 0, 640), A("st2"), scale=col(8))] if end else []]
    chain(40, 40, 280, 80, 640, pf, vf, TURN[1])

    def base2():
        for n in range(nd):
            mm(A("pH", 0, 40), A("upp"), A("fl", 120 + 40 * n, 160 + 40 * n), False, False)
            mm(A("pH", 0, 40), A("nblk"), A("sc", 80 + 40 * n, 120 + 40 * n), False, n == nd - 1)
        mm(A("pU", 8, 9), A("blk"), A("sa", 39, 40), True, False)
        for n in range(nd):
            mm(A("pU", 8, 9), A("nblk"), A("sc", 119 + 40 * n, 120 + 40 * n), False, n == nd - 1)

    def counts2():
        if rank + 2 < N:
            if nd == 1:
                act(A("ex", 32, 33), A("pC", 48, 49), Fn.Identity, bias=-64.0)
            else:
                act(A("ex", 32, 33), A("pC", 39, 40))
            send([(rank + 1, A("ex", 32, 40), A("land2", 0, 8), "ar2x")], 4)

    pack(40, 120, 80, 96, 128, 488, 640, "st2f", 256, [lambda: stays(40, 120)], [base2], [counts2],
         [lambda: tt(A("mm", 40, 80), A("pH", 0, 40), A("fl", 120 + bb, 160 + bb), Op.mult),
          lambda: ts(A("dr", 0, 4), A("jw", 0, 4), A("pU", 8, 9), Op.add, 64.0, Op.add),
          lambda: tt(A("tmp", 0, 40), A("mm", 40, 80), A("cj", 40, 80), Op.add),
          lambda: copy(A("offs", 480, 484), A("dr", 0, 4)),
          lambda: copy(A("offs", 440, 480), A("tmp", 0, 40))])
    migrate(256, "land2", ("ar2r", "ar2l"))
    scatter(A("w2"), A("offs", 440, 480), A("gk", 640, 1280), A("st2"), Op.add)
    if not end:
        arrive([A("land2", 0, 8)], "ar2x", 4)
        ts(A("offs", 484, 488), A("dr", 0, 4), A("land2", 0, 1), Op.add)
    fw = A("w2", 0, 640)
    if hasL:
        arrive([A("land2", 16, 80), A("land2", 144, 208)], "ar2l", comes(rank - 1))
        scatter(fw, A("offs", 480, 484), A("land2", 16, 80), A("land2", 144, 208), Op.add)
    if hasR:
        arrive([A("land2", 80, 144), A("land2", 208, 272)], "ar2r", comes(rank + 1))
        ro = 484 if hasL else 480
        scatter(fw, A("offs", ro, ro + 4), A("land2", 80, 144), A("land2", 208, 272), Op.add)
    conv("pA", 0, 32, ZXV, "w2", 0, True, True)
    conv("pU", 0, 32, ZW, "w2", 0, True, True)
    xo = A("pci", 64, 96)
    ts(xo, A("pA", 0, 32), 1.0 / 128, Op.mult)
    if end:
        c = 8191.0 if hasL else -1.0
        ts(A("tmp", 128, 160), xo, -1.0, Op.mult, c, Op.add)
        ts(A("tmp", 288, 320), xo, -128.0, Op.mult)
        tt(A("ox"), xo, A("tmp", 128, 160), Op.min if hasL else Op.max)
        dma("Y", T.yx[:], A("ox"))
        ts(A("tmp", 160, 192), xo, -2.0 if hasL else 2.0, Op.mult, abs(c), Op.add)
        tt(A("tmp", 192, 224), A("pA", 0, 32), A("tmp", 288, 320), Op.add)
        ts(A("tmp", 224, 256), A("tmp", 160, 192), -1.0, Op.max, 1.0, Op.min)
        tt(A("ov"), A("tmp", 192, 224), A("tmp", 224, 256), Op.mult)
    else:
        ts(A("tmp", 288, 320), xo, -128.0, Op.mult)
        copy(A("ox"), xo)
        dma("Y", T.yx[:], A("ox"))
        tt(A("ov"), A("pA", 0, 32), A("tmp", 288, 320), Op.add)
    dma("Y", T.yv[:], A("ov"))
    act(A("ow"), A("pU", 0, 32))
    dma("S", T.yw[:], A("ow"))
    emit(g, T, ops)
